import numpy as np
import ml_dtypes


def mxq(x, axis, fmt="e4m3"):
    dtype, down = {"e4m3": (ml_dtypes.float8_e4m3fn, 7), "e5m2": (ml_dtypes.float8_e5m2, 14)}[fmt]
    v = np.moveaxis(np.asarray(x, np.float32).astype(ml_dtypes.bfloat16).astype(np.float64), axis, -1)
    blocks = v.reshape(v.shape[:-1] + (-1, 32))
    amax = np.abs(blocks).max(-1, keepdims=True)
    byte = np.maximum(np.where(amax > 0, np.frexp(amax)[1] - 1 + 127, 0) - down, 1)
    scale = np.exp2(byte - 127.0)
    codes = (blocks / scale).astype(np.float32).astype(dtype).astype(np.float64)
    return np.moveaxis((codes * scale).reshape(v.shape), -1, axis)


WIDE = False


def mx_kscale(k):
    if not WIDE:
        return np.ones(k)
    levels = np.array([10, -10, 5, -5, 0])
    if k % 512:
        return np.exp2(np.random.permutation(np.resize(levels, k // 32))).repeat(32)
    a = np.empty((k // 512, 16))
    for p in range(k // 512):
        a[p, :8] = np.random.permutation(np.resize(levels, 8))
        for g in range(8):
            far = levels[np.abs(levels - a[p, g]) >= 10]
            a[p, g + 8] = far[np.random.randint(len(far))]
    return np.exp2(a.ravel()).repeat(32)


def f64(x):
    return np.asarray(x).astype(np.float64)


def striped(idx):
    return np.tile(idx.reshape(-1, 16).T, (8, 1)).astype(np.uint16)


def unstriped(offs):
    return offs[:16].T.reshape(-1).astype(np.int64)


K, T, E, C, N = 1024, 1024, 4, 128, 128


def by_expert(wq, xq):
    return np.concatenate([wq[e].T @ xq[:, e * C:(e + 1) * C] for e in range(E)], axis=1)


def setup_inputs():
    n = np.random.standard_normal
    s = mx_kscale(K)[:, None]
    return {
        "xT": (n((K, T)) * s).astype(np.float32),
        "w": (n((E, K, N)) / np.sqrt(K) / s[None]).astype(np.float32),
        "gate": np.tile(np.random.uniform(0.2, 1.0, E * C), (N, 1)).astype(np.float32),
        "offs": striped(np.random.permutation(T)[:E * C]),
    }


def reference(xT, w, gate, offs):
    idx = unstriped(offs)
    xq = mxq(f64(xT)[:, idx], 0, "e4m3")
    y = by_expert(mxq(f64(w), 1, "e4m3"), xq)
    out = np.zeros((N, T))
    out[:, idx] = f64(gate) * y
    return out

@@ -1,0 +1,171 @@
+from contextlib import ExitStack
+
+import concourse.mybir as mybir
+
+K, T, E, C, N = 1024, 1024, 4, 128, 128
+FLOPS = 2 * K * N * E * C
+
+F32 = mybir.dt.float32
+BF16 = mybir.dt.bfloat16
+U32 = mybir.dt.uint32
+U16 = mybir.dt.uint16
+U8 = mybir.dt.uint8
+FP8X4 = mybir.dt.float8_e4m3fn_x4
+MULT = mybir.AluOpType.mult
+
+P = 128
+PACK = 4
+PASSES = K // (P * PACK)
+SLOTS = E * C
+SL = 256
+NSL = SLOTS // SL
+EPS = SL // C
+
+
+def tile_routed_moe_kernel(tc, xT, w, gate, offs, out):
+    nc = tc.nc
+    with ExitStack() as ctx:
+        keep = ctx.enter_context(tc.tile_pool(name="keep", bufs=1))
+        psum = ctx.enter_context(tc.psum_pool(name="psum", bufs=1))
+
+        offsets = keep.tile([P, SLOTS // 16], U16, name="offsets")
+        nc.sync.dma_start(offsets[:], offs)
+
+        window = keep.tile([P, T], F32, name="window")
+        nc.vector.memset(window[:], 0.0)
+
+        planes_hbm = xT.rearrange("(g p t) n -> g p t n", p=P, t=PACK)
+        plane = {}
+        w_raw = {}
+
+        def load_plane(g, t):
+            plane[g, t] = keep.tile([P, T], F32, name="plane%d%d" % (g, t))
+            nc.sync.dma_start(plane[g, t][:], planes_hbm[g, :, t, :])
+
+        def load_weights(e):
+            w_raw[e] = keep.tile([P, PASSES, PACK, N], F32, name="w_raw%d" % e)
+            nc.sync.dma_start(w_raw[e][:], w[e].rearrange("(g p j) n -> p g j n", p=P, j=PACK))
+
+        for t in range(PACK):
+            load_plane(0, t)
+        load_plane(1, 0)
+        for e in range(E - 1):
+            load_weights(e)
+            load_plane(1, e + 1)
+        load_weights(E - 1)
+
+        gate_sb = keep.tile([P, SLOTS], F32, name="gate_sb")
+        nc.sync.dma_start(gate_sb[:], gate)
+
+        g4 = {}
+        xg = {}
+        xc = {}
+        xs = {}
+        for g in range(PASSES):
+            for s in range(NSL):
+                g4[g, s] = keep.tile([P, PACK, SL], F32, name="g4_%d%d" % (g, s))
+                xg[g, s] = keep.tile([P, SL, PACK], BF16, name="xg_%d%d" % (g, s), align_bytes=64)
+                xc[g, s] = keep.tile([P, SL], U32, name="xc_%d%d" % (g, s), align_bytes=64)
+                xs[g, s] = keep.tile([P, SL], U8, name="xs_%d%d" % (g, s), align_bytes=64)
+
+        def gather(g, t, s):
+            nc.vector.tensor_copy(
+                g4[g, s][:, t, :],
+                plane[g, t][:].indirect(offsets[:, s * (SL // 16) : (s + 1) * (SL // 16)]),
+            )
+
+        def interleave_tokens(g, s, engine):
+            if engine == "scalar":
+                nc.scalar.copy(xg[g, s][:], g4[g, s][:].rearrange("p t n -> p n t"))
+            else:
+                nc.vector.tensor_copy(xg[g, s][:], g4[g, s][:].rearrange("p t n -> p n t"))
+
+        def quantize_tokens(g, s):
+            nc.vector.quantize_mx(
+                out=xc[g, s][:].bitcast(FP8X4),
+                scales=xs[g, s][:],
+                in_=xg[g, s][:].rearrange("p n t -> p (n t)"),
+            )
+
+        wg = []
+        wc = []
+        ws = []
+        for e in range(E):
+            wg.append(keep.tile([P, PASSES, N, PACK], BF16, name="wg%d" % e, align_bytes=64))
+            wc.append(keep.tile([P, PASSES * N], U32, name="wc%d" % e, align_bytes=64))
+            ws.append(keep.tile([P, PASSES * N], U8, name="ws%d" % e, align_bytes=64))
+
+        def interleave_weights(e):
+            nc.scalar.copy(wg[e][:], w_raw[e][:].rearrange("p g j n -> p g n j"))
+
+        def quantize_weights(e):
+            nc.vector.quantize_mx(
+                out=wc[e][:].bitcast(FP8X4),
+                scales=ws[e][:],
+                in_=wg[e][:].rearrange("p g n j -> p (g n j)"),
+            )
+
+        acc = [psum.tile([P, SL], F32, name="acc%d" % s) for s in range(NSL)]
+        y_sb = [keep.tile([P, SL], F32, name="y_sb%d" % s) for s in range(NSL)]
+
+        def multiply(e):
+            s, c0 = e // EPS, (e % EPS) * C
+            for g in range(PASSES):
+                nc.tensor.matmul_mx(
+                    out=acc[s][:, c0 : c0 + C],
+                    lhsT=wc[e][:, g * N : (g + 1) * N].bitcast(FP8X4),
+                    lhsT_scale=ws[e][:, g * N : (g + 1) * N],
+                    rhs=xc[g, s][:, c0 : c0 + C].bitcast(FP8X4),
+                    rhs_scale=xs[g, s][:, c0 : c0 + C],
+                    start=(g == 0),
+                    stop=(g == PASSES - 1),
+                )
+
+        def sums_to_sbuf(s):
+            nc.scalar.copy(y_sb[s][:], acc[s][:])
+
+        def scatter(s):
+            nc.vector.tensor_tensor(
+                window[:].indirect(offsets[:, s * (SL // 16) : (s + 1) * (SL // 16)]),
+                y_sb[s][:],
+                gate_sb[:, s * SL : (s + 1) * SL],
+                MULT,
+            )
+
+        for t in range(PACK):
+            for s in range(NSL):
+                gather(0, t, s)
+        interleave_tokens(0, 0, "scalar")
+        gather(1, 0, 0)
+        gather(1, 0, 1)
+        interleave_tokens(0, 1, "scalar")
+        gather(1, 1, 0)
+        gather(1, 1, 1)
+        interleave_weights(0)
+        quantize_tokens(0, 0)
+        quantize_tokens(0, 1)
+        gather(1, 2, 0)
+        gather(1, 2, 1)
+        interleave_weights(1)
+        quantize_weights(0)
+        interleave_weights(2)
+        quantize_weights(1)
+        gather(1, 3, 0)
+        gather(1, 3, 1)
+        interleave_tokens(1, 0, "scalar")
+        quantize_weights(2)
+        interleave_tokens(1, 1, "vector")
+        interleave_weights(3)
+        quantize_tokens(1, 0)
+        quantize_tokens(1, 1)
+        multiply(0)
+        multiply(1)
+        multiply(2)
+        sums_to_sbuf(0)
+        quantize_weights(3)
+        multiply(3)
+        scatter(0)
+        sums_to_sbuf(1)
+        scatter(1)
+
+        nc.sync.dma_start(out, window[:])

@@ -35,68 +35,51 @@ def tile_routed_moe_kernel(tc, xT, w, gate, offs, out):
         nc.vector.memset(window[:], 0.0)
 
         planes_hbm = xT.rearrange("(g p t) n -> g p t n", p=P, t=PACK)
-        plane = {}
-        w_raw = {}
+        x_raw = [keep.tile([P, PACK, T], F32, name="x_raw%d" % g) for g in range(PASSES)]
+        w_raw = [keep.tile([P, PASSES, PACK, N], F32, name="w_raw%d" % e) for e in range(E)]
+        gate_sb = keep.tile([P, SLOTS], F32, name="gate_sb")
 
         def load_plane(g, t):
-            plane[g, t] = keep.tile([P, T], F32, name="plane%d%d" % (g, t))
-            nc.sync.dma_start(plane[g, t][:], planes_hbm[g, :, t, :])
+            nc.sync.dma_start(x_raw[g][:, t, :], planes_hbm[g, :, t, :])
 
         def load_weights(e):
-            w_raw[e] = keep.tile([P, PASSES, PACK, N], F32, name="w_raw%d" % e)
             nc.sync.dma_start(w_raw[e][:], w[e].rearrange("(g p j) n -> p g j n", p=P, j=PACK))
 
         for t in range(PACK):
             load_plane(0, t)
+        load_weights(0)
         load_plane(1, 0)
-        for e in range(E - 1):
-            load_weights(e)
-            load_plane(1, e + 1)
-        load_weights(E - 1)
-
-        gate_sb = keep.tile([P, SLOTS], F32, name="gate_sb")
+        load_plane(1, 1)
+        load_plane(1, 2)
+        load_weights(1)
+        load_plane(1, 3)
+        load_weights(2)
+        load_weights(3)
         nc.sync.dma_start(gate_sb[:], gate)
 
-        g4 = {}
-        xg = {}
-        xc = {}
-        xs = {}
-        for g in range(PASSES):
-            for s in range(NSL):
-                g4[g, s] = keep.tile([P, PACK, SL], F32, name="g4_%d%d" % (g, s))
-                xg[g, s] = keep.tile([P, SL, PACK], BF16, name="xg_%d%d" % (g, s), align_bytes=64)
-                xc[g, s] = keep.tile([P, SL], U32, name="xc_%d%d" % (g, s), align_bytes=64)
-                xs[g, s] = keep.tile([P, SL], U8, name="xs_%d%d" % (g, s), align_bytes=64)
+        xg = [keep.tile([P, SLOTS, PACK], BF16, name="xg%d" % g, align_bytes=64) for g in range(PASSES)]
+        xc = [keep.tile([P, SLOTS], U32, name="xc%d" % g, align_bytes=64) for g in range(PASSES)]
+        xs = [keep.tile([P, SLOTS], U8, name="xs%d" % g, align_bytes=64) for g in range(PASSES)]
 
-        def gather(g, t, s):
-            nc.vector.tensor_copy(
-                g4[g, s][:, t, :],
-                plane[g, t][:].indirect(offsets[:, s * (SL // 16) : (s + 1) * (SL // 16)]),
-            )
+        def gather(g, t):
+            nc.vector.tensor_copy(xg[g][:, :, t], x_raw[g][:, t, :].indirect(offsets[:]))
 
-        def interleave_tokens(g, s, engine):
-            if engine == "scalar":
-                nc.scalar.copy(xg[g, s][:], g4[g, s][:].rearrange("p t n -> p n t"))
-            else:
-                nc.vector.tensor_copy(xg[g, s][:], g4[g, s][:].rearrange("p t n -> p n t"))
-
-        def quantize_tokens(g, s):
+        def quantize_tokens(g):
             nc.vector.quantize_mx(
-                out=xc[g, s][:].bitcast(FP8X4),
-                scales=xs[g, s][:],
-                in_=xg[g, s][:].rearrange("p n t -> p (n t)"),
+                out=xc[g][:].bitcast(FP8X4),
+                scales=xs[g][:],
+                in_=xg[g][:].rearrange("p n t -> p (n t)"),
             )
 
-        wg = []
-        wc = []
-        ws = []
-        for e in range(E):
-            wg.append(keep.tile([P, PASSES, N, PACK], BF16, name="wg%d" % e, align_bytes=64))
-            wc.append(keep.tile([P, PASSES * N], U32, name="wc%d" % e, align_bytes=64))
-            ws.append(keep.tile([P, PASSES * N], U8, name="ws%d" % e, align_bytes=64))
+        wg = [keep.tile([P, PASSES, N, PACK], BF16, name="wg%d" % e, align_bytes=64) for e in range(E)]
+        wc = [keep.tile([P, PASSES * N], U32, name="wc%d" % e, align_bytes=64) for e in range(E)]
+        ws = [keep.tile([P, PASSES * N], U8, name="ws%d" % e, align_bytes=64) for e in range(E)]
 
-        def interleave_weights(e):
-            nc.scalar.copy(wg[e][:], w_raw[e][:].rearrange("p g j n -> p g n j"))
+        def interleave_weights(e, engine):
+            if engine == "scalar":
+                nc.scalar.copy(wg[e][:], w_raw[e][:].rearrange("p g j n -> p g n j"))
+            else:
+                nc.vector.tensor_copy(wg[e][:], w_raw[e][:].rearrange("p g j n -> p g n j"))
 
         def quantize_weights(e):
             nc.vector.quantize_mx(
@@ -115,8 +98,8 @@ def tile_routed_moe_kernel(tc, xT, w, gate, offs, out):
                     out=acc[s][:, c0 : c0 + C],
                     lhsT=wc[e][:, g * N : (g + 1) * N].bitcast(FP8X4),
                     lhsT_scale=ws[e][:, g * N : (g + 1) * N],
-                    rhs=xc[g, s][:, c0 : c0 + C].bitcast(FP8X4),
-                    rhs_scale=xs[g, s][:, c0 : c0 + C],
+                    rhs=xc[g][:, e * C : (e + 1) * C].bitcast(FP8X4),
+                    rhs_scale=xs[g][:, e * C : (e + 1) * C],
                     start=(g == 0),
                     stop=(g == PASSES - 1),
                 )
@@ -133,36 +116,25 @@ def tile_routed_moe_kernel(tc, xT, w, gate, offs, out):
             )
 
         for t in range(PACK):
-            for s in range(NSL):
-                gather(0, t, s)
-        interleave_tokens(0, 0, "scalar")
-        gather(1, 0, 0)
-        gather(1, 0, 1)
-        interleave_tokens(0, 1, "scalar")
-        gather(1, 1, 0)
-        gather(1, 1, 1)
-        interleave_weights(0)
-        quantize_tokens(0, 0)
-        quantize_tokens(0, 1)
-        gather(1, 2, 0)
-        gather(1, 2, 1)
-        interleave_weights(1)
+            gather(0, t)
+        interleave_weights(0, "scalar")
+        quantize_tokens(0)
+        gather(1, 0)
+        gather(1, 1)
+        gather(1, 2)
+        interleave_weights(1, "scalar")
         quantize_weights(0)
-        interleave_weights(2)
+        gather(1, 3)
+        interleave_weights(2, "scalar")
         quantize_weights(1)
-        gather(1, 3, 0)
-        gather(1, 3, 1)
-        interleave_tokens(1, 0, "scalar")
-        quantize_weights(2)
-        interleave_tokens(1, 1, "vector")
-        interleave_weights(3)
-        quantize_tokens(1, 0)
-        quantize_tokens(1, 1)
+        quantize_tokens(1)
+        interleave_weights(3, "vector")
         multiply(0)
         multiply(1)
-        multiply(2)
         sums_to_sbuf(0)
+        quantize_weights(2)
         quantize_weights(3)
+        multiply(2)
         multiply(3)
         scatter(0)
         sums_to_sbuf(1)

@@ -35,20 +35,24 @@ def tile_routed_moe_kernel(tc, xT, w, gate, offs, out):
         nc.vector.memset(window[:], 0.0)
 
         planes_hbm = xT.rearrange("(g p t) n -> g p t n", p=P, t=PACK)
-        x_raw = [keep.tile([P, PACK, T], F32, name="x_raw%d" % g) for g in range(PASSES)]
-        w_raw = [keep.tile([P, PASSES, PACK, N], F32, name="w_raw%d" % e) for e in range(E)]
+        plane = {}
+        w_raw = {}
         gate_sb = keep.tile([P, SLOTS], F32, name="gate_sb")
 
         def load_plane(g, t):
-            nc.sync.dma_start(x_raw[g][:, t, :], planes_hbm[g, :, t, :])
+            plane[g, t] = keep.tile([P, T], F32, name="plane%d%d" % (g, t))
+            nc.sync.dma_start(plane[g, t][:], planes_hbm[g, :, t, :])
 
         def load_weights(e):
+            w_raw[e] = keep.tile([P, PASSES, PACK, N], F32, name="w_raw%d" % e)
             nc.sync.dma_start(w_raw[e][:], w[e].rearrange("(g p j) n -> p g j n", p=P, j=PACK))
 
-        for t in range(PACK):
-            load_plane(0, t)
-        load_weights(0)
+        load_plane(0, 0)
+        load_plane(0, 1)
+        load_plane(0, 2)
+        load_plane(0, 3)
         load_plane(1, 0)
+        load_weights(0)
         load_plane(1, 1)
         load_plane(1, 2)
         load_weights(1)
@@ -57,23 +61,43 @@ def tile_routed_moe_kernel(tc, xT, w, gate, offs, out):
         load_weights(3)
         nc.sync.dma_start(gate_sb[:], gate)
 
-        xg = [keep.tile([P, SLOTS, PACK], BF16, name="xg%d" % g, align_bytes=64) for g in range(PASSES)]
-        xc = [keep.tile([P, SLOTS], U32, name="xc%d" % g, align_bytes=64) for g in range(PASSES)]
-        xs = [keep.tile([P, SLOTS], U8, name="xs%d" % g, align_bytes=64) for g in range(PASSES)]
+        g4 = {}
+        xg = {}
+        xc = {}
+        xs = {}
+        for g in range(PASSES):
+            for s in range(NSL):
+                g4[g, s] = keep.tile([P, PACK, SL], F32, name="g4_%d%d" % (g, s))
+                xg[g, s] = keep.tile([P, SL, PACK], BF16, name="xg_%d%d" % (g, s), align_bytes=64)
+                xc[g, s] = keep.tile([P, SL], U32, name="xc_%d%d" % (g, s), align_bytes=64)
+                xs[g, s] = keep.tile([P, SL], U8, name="xs_%d%d" % (g, s), align_bytes=64)
 
-        def gather(g, t):
-            nc.vector.tensor_copy(xg[g][:, :, t], x_raw[g][:, t, :].indirect(offsets[:]))
-
-        def quantize_tokens(g):
-            nc.vector.quantize_mx(
-                out=xc[g][:].bitcast(FP8X4),
-                scales=xs[g][:],
-                in_=xg[g][:].rearrange("p n t -> p (n t)"),
+        def gather(g, t, s):
+            nc.vector.tensor_copy(
+                g4[g, s][:, t, :],
+                plane[g, t][:].indirect(offsets[:, s * (SL // 16) : (s + 1) * (SL // 16)]),
             )
 
-        wg = [keep.tile([P, PASSES, N, PACK], BF16, name="wg%d" % e, align_bytes=64) for e in range(E)]
-        wc = [keep.tile([P, PASSES * N], U32, name="wc%d" % e, align_bytes=64) for e in range(E)]
-        ws = [keep.tile([P, PASSES * N], U8, name="ws%d" % e, align_bytes=64) for e in range(E)]
+        def interleave_tokens(g, s, engine):
+            if engine == "scalar":
+                nc.scalar.copy(xg[g, s][:], g4[g, s][:].rearrange("p t n -> p n t"))
+            else:
+                nc.vector.tensor_copy(xg[g, s][:], g4[g, s][:].rearrange("p t n -> p n t"))
+
+        def quantize_tokens(g, s):
+            nc.vector.quantize_mx(
+                out=xc[g, s][:].bitcast(FP8X4),
+                scales=xs[g, s][:],
+                in_=xg[g, s][:].rearrange("p n t -> p (n t)"),
+            )
+
+        wg = []
+        wc = []
+        ws = []
+        for e in range(E):
+            wg.append(keep.tile([P, PASSES, N, PACK], BF16, name="wg%d" % e, align_bytes=64))
+            wc.append(keep.tile([P, PASSES * N], U32, name="wc%d" % e, align_bytes=64))
+            ws.append(keep.tile([P, PASSES * N], U8, name="ws%d" % e, align_bytes=64))
 
         def interleave_weights(e, engine):
             if engine == "scalar":
@@ -98,8 +122,8 @@ def tile_routed_moe_kernel(tc, xT, w, gate, offs, out):
                     out=acc[s][:, c0 : c0 + C],
                     lhsT=wc[e][:, g * N : (g + 1) * N].bitcast(FP8X4),
                     lhsT_scale=ws[e][:, g * N : (g + 1) * N],
-                    rhs=xc[g][:, e * C : (e + 1) * C].bitcast(FP8X4),
-                    rhs_scale=xs[g][:, e * C : (e + 1) * C],
+                    rhs=xc[g, s][:, c0 : c0 + C].bitcast(FP8X4),
+                    rhs_scale=xs[g, s][:, c0 : c0 + C],
                     start=(g == 0),
                     stop=(g == PASSES - 1),
                 )
@@ -115,22 +139,38 @@ def tile_routed_moe_kernel(tc, xT, w, gate, offs, out):
                 MULT,
             )
 
-        for t in range(PACK):
-            gather(0, t)
+        gather(0, 0, 0)
+        gather(0, 0, 1)
+        gather(0, 1, 0)
+        gather(0, 1, 1)
+        gather(0, 2, 0)
+        gather(0, 2, 1)
+        gather(0, 3, 0)
+        gather(0, 3, 1)
+        interleave_tokens(0, 0, "scalar")
+        gather(1, 0, 0)
+        gather(1, 0, 1)
+        interleave_tokens(0, 1, "scalar")
+        quantize_tokens(0, 0)
+        gather(1, 1, 0)
         interleave_weights(0, "scalar")
-        quantize_tokens(0)
-        gather(1, 0)
-        gather(1, 1)
-        gather(1, 2)
+        gather(1, 1, 1)
+        gather(1, 2, 0)
         interleave_weights(1, "scalar")
+        gather(1, 2, 1)
+        quantize_tokens(0, 1)
         quantize_weights(0)
-        gather(1, 3)
-        interleave_weights(2, "scalar")
+        gather(1, 3, 0)
+        gather(1, 3, 1)
+        interleave_tokens(1, 0, "scalar")
         quantize_weights(1)
-        quantize_tokens(1)
-        interleave_weights(3, "vector")
+        interleave_tokens(1, 1, "vector")
+        interleave_weights(2, "scalar")
+        quantize_tokens(1, 0)
+        quantize_tokens(1, 1)
         multiply(0)
         multiply(1)
+        interleave_weights(3, "vector")
         sums_to_sbuf(0)
         quantize_weights(2)
         quantize_weights(3)

@@ -80,9 +80,9 @@ def tile_routed_moe_kernel(tc, xT, w, gate, offs, out):
 
         def interleave_tokens(g, s, engine):
             if engine == "scalar":
-                nc.scalar.copy(xg[g, s][:], g4[g, s][:].rearrange("p t n -> p n t"))
+                nc.scalar.copy(xg[g, s][:].rearrange("p (c i) t -> p c t i", i=4), g4[g, s][:].rearrange("p t (c i) -> p c t i", i=4))
             else:
-                nc.vector.tensor_copy(xg[g, s][:], g4[g, s][:].rearrange("p t n -> p n t"))
+                nc.vector.tensor_copy(xg[g, s][:].rearrange("p (c i) t -> p c t i", i=4), g4[g, s][:].rearrange("p t (c i) -> p c t i", i=4))
 
         def quantize_tokens(g, s):
             nc.vector.quantize_mx(
@@ -100,10 +100,11 @@ def tile_routed_moe_kernel(tc, xT, w, gate, offs, out):
             ws.append(keep.tile([P, PASSES * N], U8, name="ws%d" % e, align_bytes=64))
 
         def interleave_weights(e, engine):
-            if engine == "scalar":
-                nc.scalar.copy(wg[e][:], w_raw[e][:].rearrange("p g j n -> p g n j"))
-            else:
-                nc.vector.tensor_copy(wg[e][:], w_raw[e][:].rearrange("p g j n -> p g n j"))
+            for g in range(PASSES):
+                if engine == "scalar":
+                    nc.scalar.copy(wg[e][:, g].rearrange("p (c i) j -> p c j i", i=4), w_raw[e][:, g].rearrange("p j (c i) -> p c j i", i=4))
+                else:
+                    nc.vector.tensor_copy(wg[e][:, g].rearrange("p (c i) j -> p c j i", i=4), w_raw[e][:, g].rearrange("p j (c i) -> p c j i", i=4))
 
         def quantize_weights(e):
             nc.vector.quantize_mx(

@@ -20,6 +20,8 @@ SLOTS = E * C
 SL = 256
 NSL = SLOTS // SL
 EPS = SL // C
+LINE = 4
+WIDE = 2 * T
 
 
 def tile_routed_moe_kernel(tc, xT, w, gate, offs, out):
@@ -40,8 +42,8 @@ def tile_routed_moe_kernel(tc, xT, w, gate, offs, out):
         gate_sb = keep.tile([P, SLOTS], F32, name="gate_sb")
 
         def load_plane(g, t):
-            plane[g, t] = keep.tile([P, T], F32, name="plane%d%d" % (g, t))
-            nc.sync.dma_start(plane[g, t][:], planes_hbm[g, :, t, :])
+            plane[g, t] = keep.tile([P, T if t == PACK - 1 else WIDE], F32, name="plane%d%d" % (g, t))
+            nc.sync.dma_start(plane[g, t][:, 0:T], planes_hbm[g, :, t, :])
 
         def load_weights(e):
             w_raw[e] = keep.tile([P, PASSES, PACK, N], F32, name="w_raw%d" % e)
@@ -61,28 +63,35 @@ def tile_routed_moe_kernel(tc, xT, w, gate, offs, out):
         load_weights(3)
         nc.sync.dma_start(gate_sb[:], gate)
 
-        g4 = {}
+        g4 = [keep.tile([P, PACK, SLOTS], F32, name="g4_%d" % g) for g in range(PASSES)]
         xg = {}
         xc = {}
         xs = {}
         for g in range(PASSES):
             for s in range(NSL):
-                g4[g, s] = keep.tile([P, PACK, SL], F32, name="g4_%d%d" % (g, s))
                 xg[g, s] = keep.tile([P, SL, PACK], BF16, name="xg_%d%d" % (g, s), align_bytes=64)
                 xc[g, s] = keep.tile([P, SL], U32, name="xc_%d%d" % (g, s), align_bytes=64)
                 xs[g, s] = keep.tile([P, SL], U8, name="xs_%d%d" % (g, s), align_bytes=64)
 
+        def gather_all(g, t):
+            nc.vector.tensor_copy(g4[g][:, t, :], plane[g, t][:].indirect(offsets[:]))
+
         def gather(g, t, s):
             nc.vector.tensor_copy(
-                g4[g, s][:, t, :],
+                g4[g][:, t, s * SL : (s + 1) * SL],
                 plane[g, t][:].indirect(offsets[:, s * (SL // 16) : (s + 1) * (SL // 16)]),
             )
 
-        def interleave_tokens(g, s, engine):
+        def copy_on(engine, dst, src):
             if engine == "scalar":
-                nc.scalar.copy(xg[g, s][:].rearrange("p (c i) t -> p c t i", i=4), g4[g, s][:].rearrange("p t (c i) -> p c t i", i=4))
+                nc.scalar.copy(dst, src)
             else:
-                nc.vector.tensor_copy(xg[g, s][:].rearrange("p (c i) t -> p c t i", i=4), g4[g, s][:].rearrange("p t (c i) -> p c t i", i=4))
+                nc.vector.tensor_copy(dst, src)
+
+        def interleave_tokens(g, s, engine):
+            dst = xg[g, s][:].rearrange("p (c i) t -> p c t i", i=LINE)
+            src = g4[g][:, :, s * SL : (s + 1) * SL].rearrange("p t (c i) -> p c t i", i=LINE)
+            copy_on(engine, dst, src)
 
         def quantize_tokens(g, s):
             nc.vector.quantize_mx(
@@ -101,10 +110,9 @@ def tile_routed_moe_kernel(tc, xT, w, gate, offs, out):
 
         def interleave_weights(e, engine):
             for g in range(PASSES):
-                if engine == "scalar":
-                    nc.scalar.copy(wg[e][:, g].rearrange("p (c i) j -> p c j i", i=4), w_raw[e][:, g].rearrange("p j (c i) -> p c j i", i=4))
-                else:
-                    nc.vector.tensor_copy(wg[e][:, g].rearrange("p (c i) j -> p c j i", i=4), w_raw[e][:, g].rearrange("p j (c i) -> p c j i", i=4))
+                dst = wg[e][:, g].rearrange("p (c i) j -> p c j i", i=LINE)
+                src = w_raw[e][:, g].rearrange("p j (c i) -> p c j i", i=LINE)
+                copy_on(engine, dst, src)
 
         def quantize_weights(e):
             nc.vector.quantize_mx(
@@ -140,25 +148,19 @@ def tile_routed_moe_kernel(tc, xT, w, gate, offs, out):
                 MULT,
             )
 
-        gather(0, 0, 0)
-        gather(0, 0, 1)
-        gather(0, 1, 0)
-        gather(0, 1, 1)
-        gather(0, 2, 0)
-        gather(0, 2, 1)
+        gather_all(0, 0)
+        gather_all(0, 1)
+        gather_all(0, 2)
         gather(0, 3, 0)
         gather(0, 3, 1)
         interleave_tokens(0, 0, "scalar")
-        gather(1, 0, 0)
-        gather(1, 0, 1)
+        gather_all(1, 0)
         interleave_tokens(0, 1, "scalar")
         quantize_tokens(0, 0)
-        gather(1, 1, 0)
+        gather_all(1, 1)
         interleave_weights(0, "scalar")
-        gather(1, 1, 1)
-        gather(1, 2, 0)
+        gather_all(1, 2)
         interleave_weights(1, "scalar")
-        gather(1, 2, 1)
         quantize_tokens(0, 1)
         quantize_weights(0)
         gather(1, 3, 0)

@@ -93,6 +93,17 @@ def tile_routed_moe_kernel(tc, xT, w, gate, offs, out):
             src = g4[g][:, :, s * SL : (s + 1) * SL].rearrange("p t (c i) -> p c t i", i=LINE)
             copy_on(engine, dst, src)
 
+        def interleave_three(g, s):
+            dst = xg[g, s][:, :, 0 : PACK - 1].rearrange("p (c i) t -> p c t i", i=LINE)
+            src = g4[g][:, 0 : PACK - 1, s * SL : (s + 1) * SL].rearrange("p t (c i) -> p c t i", i=LINE)
+            nc.vector.tensor_copy(dst, src)
+
+        def gather_straight(g, t, s):
+            nc.vector.tensor_copy(
+                xg[g, s][:, :, t],
+                plane[g, t][:].indirect(offsets[:, s * (SL // 16) : (s + 1) * (SL // 16)]),
+            )
+
         def quantize_tokens(g, s):
             nc.vector.quantize_mx(
                 out=xc[g, s][:].bitcast(FP8X4),
@@ -161,16 +172,16 @@ def tile_routed_moe_kernel(tc, xT, w, gate, offs, out):
         interleave_weights(0, "scalar")
         gather_all(1, 2)
         interleave_weights(1, "scalar")
+        interleave_three(1, 1)
         quantize_tokens(0, 1)
         quantize_weights(0)
         gather(1, 3, 0)
-        gather(1, 3, 1)
+        gather_straight(1, 3, 1)
         interleave_tokens(1, 0, "scalar")
         quantize_weights(1)
-        interleave_tokens(1, 1, "vector")
+        quantize_tokens(1, 1)
         interleave_weights(2, "scalar")
         quantize_tokens(1, 0)
-        quantize_tokens(1, 1)
         multiply(0)
         multiply(1)
         interleave_weights(3, "vector")

@@ -54,8 +54,8 @@ def tile_routed_moe_kernel(tc, xT, w, gate, offs, out):
         load_plane(0, 2)
         load_plane(0, 3)
         load_plane(1, 0)
-        load_weights(0)
         load_plane(1, 1)
+        load_weights(0)
         load_plane(1, 2)
         load_weights(1)
         load_plane(1, 3)
@@ -167,21 +167,21 @@ def tile_routed_moe_kernel(tc, xT, w, gate, offs, out):
         interleave_tokens(0, 0, "scalar")
         gather_all(1, 0)
         interleave_tokens(0, 1, "scalar")
-        quantize_tokens(0, 0)
         gather_all(1, 1)
+        quantize_tokens(0, 0)
         interleave_weights(0, "scalar")
-        gather_all(1, 2)
-        interleave_weights(1, "scalar")
-        interleave_three(1, 1)
         quantize_tokens(0, 1)
+        gather_all(1, 2)
+        interleave_three(1, 0)
+        interleave_three(1, 1)
+        interleave_weights(1, "scalar")
         quantize_weights(0)
-        gather(1, 3, 0)
+        gather_straight(1, 3, 0)
         gather_straight(1, 3, 1)
-        interleave_tokens(1, 0, "scalar")
         quantize_weights(1)
+        quantize_tokens(1, 0)
         quantize_tokens(1, 1)
         interleave_weights(2, "scalar")
-        quantize_tokens(1, 0)
         multiply(0)
         multiply(1)
         interleave_weights(3, "vector")

@@ -12,6 +12,7 @@ U16 = mybir.dt.uint16
 U8 = mybir.dt.uint8
 FP8X4 = mybir.dt.float8_e4m3fn_x4
 MULT = mybir.AluOpType.mult
+COPY = mybir.ActivationFunctionType.Copy
 
 P = 128
 PACK = 4
@@ -21,7 +22,7 @@ SL = 256
 NSL = SLOTS // SL
 EPS = SL // C
 LINE = 4
-WIDE = 2 * T
+SCATTERS = ((0,), (1,), (2,), (3,))
 
 
 def tile_routed_moe_kernel(tc, xT, w, gate, offs, out):
@@ -42,26 +43,29 @@ def tile_routed_moe_kernel(tc, xT, w, gate, offs, out):
         gate_sb = keep.tile([P, SLOTS], F32, name="gate_sb")
 
         def load_plane(g, t):
-            plane[g, t] = keep.tile([P, T if t == PACK - 1 else WIDE], F32, name="plane%d%d" % (g, t))
-            nc.sync.dma_start(plane[g, t][:, 0:T], planes_hbm[g, :, t, :])
+            plane[g, t] = keep.tile([P, T], F32, name="plane%d%d" % (g, t))
+            nc.sync.dma_start(plane[g, t][:], planes_hbm[g, :, t, :])
 
         def load_weights(e):
-            w_raw[e] = keep.tile([P, PASSES, PACK, N], F32, name="w_raw%d" % e)
+            w_raw[e] = keep.tile([P, PASSES, PACK, N], F32, name="w_raw%d" % e, tag="w_raw%d" % e)
             nc.sync.dma_start(w_raw[e][:], w[e].rearrange("(g p j) n -> p g j n", p=P, j=PACK))
 
-        load_plane(0, 0)
+        def load_gate():
+            nc.sync.dma_start(gate_sb[:], gate)
+
         load_plane(0, 1)
         load_plane(0, 2)
         load_plane(0, 3)
-        load_plane(1, 0)
         load_plane(1, 1)
-        load_weights(0)
+        load_plane(1, 0)
         load_plane(1, 2)
-        load_weights(1)
+        load_plane(0, 0)
         load_plane(1, 3)
+        load_weights(0)
         load_weights(2)
         load_weights(3)
-        nc.sync.dma_start(gate_sb[:], gate)
+        load_gate()
+        load_weights(1)
 
         g4 = [keep.tile([P, PACK, SLOTS], F32, name="g4_%d" % g) for g in range(PASSES)]
         xg = {}
@@ -73,36 +77,39 @@ def tile_routed_moe_kernel(tc, xT, w, gate, offs, out):
                 xc[g, s] = keep.tile([P, SL], U32, name="xc_%d%d" % (g, s), align_bytes=64)
                 xs[g, s] = keep.tile([P, SL], U8, name="xs_%d%d" % (g, s), align_bytes=64)
 
+        def list_slice(s):
+            return offsets[:, s * (SL // 16) : (s + 1) * (SL // 16)]
+
         def gather_all(g, t):
             nc.vector.tensor_copy(g4[g][:, t, :], plane[g, t][:].indirect(offsets[:]))
 
         def gather(g, t, s):
-            nc.vector.tensor_copy(
-                g4[g][:, t, s * SL : (s + 1) * SL],
-                plane[g, t][:].indirect(offsets[:, s * (SL // 16) : (s + 1) * (SL // 16)]),
-            )
+            nc.vector.tensor_copy(g4[g][:, t, s * SL : (s + 1) * SL], plane[g, t][:].indirect(list_slice(s)))
+
+        def gather_straight(g, t, s):
+            nc.vector.tensor_copy(xg[g, s][:, :, t], plane[g, t][:].indirect(list_slice(s)))
+
+        rounded = {}
+
+        def round_plane(g, t, engine):
+            rounded[g, t] = keep.tile([P, T], BF16, name="rounded%d%d" % (g, t))
+            copy_on(engine, rounded[g, t][:], plane[g, t][:])
+
+        def gather_on_scalar(g, t, s):
+            nc.scalar.activation(xg[g, s][:, :, t], rounded[g, t][:].indirect(list_slice(s)), COPY)
 
         def copy_on(engine, dst, src):
             if engine == "scalar":
                 nc.scalar.copy(dst, src)
+            elif engine == "gpsimd":
+                nc.gpsimd.tensor_copy(dst, src)
             else:
                 nc.vector.tensor_copy(dst, src)
 
-        def interleave_tokens(g, s, engine):
-            dst = xg[g, s][:].rearrange("p (c i) t -> p c t i", i=LINE)
-            src = g4[g][:, :, s * SL : (s + 1) * SL].rearrange("p t (c i) -> p c t i", i=LINE)
+        def interleave_tokens(g, s, engine, t0=0, t1=PACK):
+            dst = xg[g, s][:, :, t0:t1].rearrange("p (c i) t -> p c t i", i=LINE)
+            src = g4[g][:, t0:t1, s * SL : (s + 1) * SL].rearrange("p t (c i) -> p c t i", i=LINE)
             copy_on(engine, dst, src)
-
-        def interleave_three(g, s):
-            dst = xg[g, s][:, :, 0 : PACK - 1].rearrange("p (c i) t -> p c t i", i=LINE)
-            src = g4[g][:, 0 : PACK - 1, s * SL : (s + 1) * SL].rearrange("p t (c i) -> p c t i", i=LINE)
-            nc.vector.tensor_copy(dst, src)
-
-        def gather_straight(g, t, s):
-            nc.vector.tensor_copy(
-                xg[g, s][:, :, t],
-                plane[g, t][:].indirect(offsets[:, s * (SL // 16) : (s + 1) * (SL // 16)]),
-            )
 
         def quantize_tokens(g, s):
             nc.vector.quantize_mx(
@@ -125,6 +132,11 @@ def tile_routed_moe_kernel(tc, xT, w, gate, offs, out):
                 src = w_raw[e][:, g].rearrange("p j (c i) -> p c j i", i=LINE)
                 copy_on(engine, dst, src)
 
+        def interleave_half(e, g, engine):
+            dst = wg[e][:, g].rearrange("p (c i) j -> p c j i", i=LINE)
+            src = w_raw[e][:, g].rearrange("p j (c i) -> p c j i", i=LINE)
+            copy_on(engine, dst, src)
+
         def quantize_weights(e):
             nc.vector.quantize_mx(
                 out=wc[e][:].bitcast(FP8X4),
@@ -132,14 +144,19 @@ def tile_routed_moe_kernel(tc, xT, w, gate, offs, out):
                 in_=wg[e][:].rearrange("p g n j -> p (g n j)"),
             )
 
-        acc = [psum.tile([P, SL], F32, name="acc%d" % s) for s in range(NSL)]
-        y_sb = [keep.tile([P, SL], F32, name="y_sb%d" % s) for s in range(NSL)]
+        acc = {}
+        y_sb = {}
+        home = {}
+        for experts in SCATTERS:
+            acc[experts] = psum.tile([P, len(experts) * C], F32, name="acc%d" % experts[0])
+            for i, e in enumerate(experts):
+                home[e] = acc[experts][:, i * C : (i + 1) * C]
 
         def multiply(e):
             s, c0 = e // EPS, (e % EPS) * C
             for g in range(PASSES):
                 nc.tensor.matmul_mx(
-                    out=acc[s][:, c0 : c0 + C],
+                    out=home[e],
                     lhsT=wc[e][:, g * N : (g + 1) * N].bitcast(FP8X4),
                     lhsT_scale=ws[e][:, g * N : (g + 1) * N],
                     rhs=xc[g, s][:, c0 : c0 + C].bitcast(FP8X4),
@@ -148,50 +165,56 @@ def tile_routed_moe_kernel(tc, xT, w, gate, offs, out):
                     stop=(g == PASSES - 1),
                 )
 
-        def sums_to_sbuf(s):
-            nc.scalar.copy(y_sb[s][:], acc[s][:])
+        def sums_to_sbuf(experts, behind=None, engine="scalar"):
+            tag = "sums%d" % experts[0] if behind is None else "w_raw%d" % behind
+            y_sb[experts] = keep.tile([P, len(experts) * C], F32, name="y_sb%d" % experts[0], tag=tag)
+            copy_on(engine, y_sb[experts][:], acc[experts][:])
 
-        def scatter(s):
+        def scatter(experts):
+            j0, j1 = experts[0] * C, (experts[-1] + 1) * C
             nc.vector.tensor_tensor(
-                window[:].indirect(offsets[:, s * (SL // 16) : (s + 1) * (SL // 16)]),
-                y_sb[s][:],
-                gate_sb[:, s * SL : (s + 1) * SL],
-                MULT,
+                window[:].indirect(offsets[:, j0 // 16 : j1 // 16]), y_sb[experts][:], gate_sb[:, j0:j1], MULT
             )
 
-        gather_all(0, 0)
         gather_all(0, 1)
         gather_all(0, 2)
-        gather(0, 3, 0)
-        gather(0, 3, 1)
-        interleave_tokens(0, 0, "scalar")
-        gather_all(1, 0)
-        interleave_tokens(0, 1, "scalar")
+        gather_all(0, 3)
+        interleave_tokens(0, 0, "scalar", 1, 4)
+        interleave_tokens(0, 1, "scalar", 1, 4)
         gather_all(1, 1)
-        quantize_tokens(0, 0)
-        interleave_weights(0, "scalar")
-        quantize_tokens(0, 1)
-        gather_all(1, 2)
-        interleave_three(1, 0)
-        interleave_three(1, 1)
-        interleave_weights(1, "scalar")
-        quantize_weights(0)
+        gather_all(1, 0)
+        gather(1, 2, 0)
+        gather(1, 2, 1)
+        interleave_tokens(1, 0, "vector", 0, 3)
+        interleave_tokens(1, 1, "vector", 0, 3)
+        round_plane(0, 0, "scalar")
+        gather_on_scalar(0, 0, 0)
+        gather_on_scalar(0, 0, 1)
         gather_straight(1, 3, 0)
         gather_straight(1, 3, 1)
-        quantize_weights(1)
+        quantize_tokens(0, 0)
         quantize_tokens(1, 0)
+        quantize_tokens(0, 1)
         quantize_tokens(1, 1)
-        interleave_weights(2, "scalar")
-        multiply(0)
-        multiply(1)
-        interleave_weights(3, "vector")
-        sums_to_sbuf(0)
+        interleave_weights(0, "scalar")
+        interleave_weights(2, "vector")
+        quantize_weights(0)
         quantize_weights(2)
-        quantize_weights(3)
+        multiply(0)
         multiply(2)
+        interleave_weights(3, "vector")
+        sums_to_sbuf((0,))
+        sums_to_sbuf((2,), behind=3)
+        interleave_weights(1, "scalar")
+        quantize_weights(3)
         multiply(3)
-        scatter(0)
-        sums_to_sbuf(1)
-        scatter(1)
+        sums_to_sbuf((3,), behind=1)
+        quantize_weights(1)
+        multiply(1)
+        sums_to_sbuf((1,))
+        scatter((0,))
+        scatter((2,))
+        scatter((3,))
+        scatter((1,))
 
         nc.sync.dma_start(out, window[:])

@@ -44,7 +44,8 @@ def tile_routed_moe_kernel(tc, xT, w, gate, offs, out):
 
         def load_plane(g, t):
             plane[g, t] = keep.tile([P, T], F32, name="plane%d%d" % (g, t))
-            nc.sync.dma_start(plane[g, t][:], planes_hbm[g, :, t, :])
+            queue = nc.scalar if (g, t) == (0, 1) else nc.sync
+            queue.dma_start(plane[g, t][:], planes_hbm[g, :, t, :])
 
         def load_weights(e):
             w_raw[e] = keep.tile([P, PASSES, PACK, N], F32, name="w_raw%d" % e, tag="w_raw%d" % e)

@@ -22,7 +22,7 @@ SL = 256
 NSL = SLOTS // SL
 EPS = SL // C
 LINE = 4
-SCATTERS = ((0,), (1,), (2,), (3,))
+SCATTERS = ((0, 1), (2, 3))
 
 
 def tile_routed_moe_kernel(tc, xT, w, gate, offs, out):
@@ -48,7 +48,7 @@ def tile_routed_moe_kernel(tc, xT, w, gate, offs, out):
             queue.dma_start(plane[g, t][:], planes_hbm[g, :, t, :])
 
         def load_weights(e):
-            w_raw[e] = keep.tile([P, PASSES, PACK, N], F32, name="w_raw%d" % e, tag="w_raw%d" % e)
+            w_raw[e] = keep.tile([P, PASSES, PACK, N], F32, name="w_raw%d" % e)
             nc.sync.dma_start(w_raw[e][:], w[e].rearrange("(g p j) n -> p g j n", p=P, j=PACK))
 
         def load_gate():
@@ -57,16 +57,16 @@ def tile_routed_moe_kernel(tc, xT, w, gate, offs, out):
         load_plane(0, 1)
         load_plane(0, 2)
         load_plane(0, 3)
-        load_plane(1, 1)
         load_plane(1, 0)
+        load_plane(1, 1)
         load_plane(1, 2)
         load_plane(0, 0)
         load_plane(1, 3)
         load_weights(0)
+        load_weights(1)
         load_weights(2)
         load_weights(3)
         load_gate()
-        load_weights(1)
 
         g4 = [keep.tile([P, PACK, SLOTS], F32, name="g4_%d" % g) for g in range(PASSES)]
         xg = {}
@@ -128,10 +128,9 @@ def tile_routed_moe_kernel(tc, xT, w, gate, offs, out):
             ws.append(keep.tile([P, PASSES * N], U8, name="ws%d" % e, align_bytes=64))
 
         def interleave_weights(e, engine):
-            for g in range(PASSES):
-                dst = wg[e][:, g].rearrange("p (c i) j -> p c j i", i=LINE)
-                src = w_raw[e][:, g].rearrange("p j (c i) -> p c j i", i=LINE)
-                copy_on(engine, dst, src)
+            dst = wg[e][:].rearrange("p g (c i) j -> p g c j i", i=LINE)
+            src = w_raw[e][:].rearrange("p g j (c i) -> p g c j i", i=LINE)
+            copy_on(engine, dst, src)
 
         def interleave_half(e, g, engine):
             dst = wg[e][:, g].rearrange("p (c i) j -> p c j i", i=LINE)
@@ -150,6 +149,7 @@ def tile_routed_moe_kernel(tc, xT, w, gate, offs, out):
         home = {}
         for experts in SCATTERS:
             acc[experts] = psum.tile([P, len(experts) * C], F32, name="acc%d" % experts[0])
+            y_sb[experts] = keep.tile([P, len(experts) * C], F32, name="y_sb%d" % experts[0])
             for i, e in enumerate(experts):
                 home[e] = acc[experts][:, i * C : (i + 1) * C]
 
@@ -166,9 +166,7 @@ def tile_routed_moe_kernel(tc, xT, w, gate, offs, out):
                     stop=(g == PASSES - 1),
                 )
 
-        def sums_to_sbuf(experts, behind=None, engine="scalar"):
-            tag = "sums%d" % experts[0] if behind is None else "w_raw%d" % behind
-            y_sb[experts] = keep.tile([P, len(experts) * C], F32, name="y_sb%d" % experts[0], tag=tag)
+        def sums_to_sbuf(experts, engine="scalar"):
             copy_on(engine, y_sb[experts][:], acc[experts][:])
 
         def scatter(experts):
@@ -180,10 +178,10 @@ def tile_routed_moe_kernel(tc, xT, w, gate, offs, out):
         gather_all(0, 1)
         gather_all(0, 2)
         gather_all(0, 3)
-        interleave_tokens(0, 0, "scalar", 1, 4)
         interleave_tokens(0, 1, "scalar", 1, 4)
-        gather_all(1, 1)
+        interleave_tokens(0, 0, "scalar", 1, 4)
         gather_all(1, 0)
+        gather_all(1, 1)
         gather(1, 2, 0)
         gather(1, 2, 1)
         interleave_tokens(1, 0, "vector", 0, 3)
@@ -198,24 +196,20 @@ def tile_routed_moe_kernel(tc, xT, w, gate, offs, out):
         quantize_tokens(0, 1)
         quantize_tokens(1, 1)
         interleave_weights(0, "scalar")
-        interleave_weights(2, "vector")
+        interleave_weights(1, "vector")
         quantize_weights(0)
-        quantize_weights(2)
-        multiply(0)
-        multiply(2)
-        interleave_weights(3, "vector")
-        sums_to_sbuf((0,))
-        sums_to_sbuf((2,), behind=3)
-        interleave_weights(1, "scalar")
-        quantize_weights(3)
-        multiply(3)
-        sums_to_sbuf((3,), behind=1)
         quantize_weights(1)
+        multiply(0)
         multiply(1)
-        sums_to_sbuf((1,))
-        scatter((0,))
-        scatter((2,))
-        scatter((3,))
-        scatter((1,))
+        interleave_weights(2, "scalar")
+        interleave_weights(3, "vector")
+        sums_to_sbuf((0, 1), "scalar")
+        quantize_weights(2)
+        quantize_weights(3)
+        multiply(2)
+        multiply(3)
+        sums_to_sbuf((2, 3), "scalar")
+        scatter((0, 1))
+        scatter((2, 3))
 
         nc.sync.dma_start(out, window[:])

@@ -51,6 +51,11 @@ def tile_routed_moe_kernel(tc, xT, w, gate, offs, out):
             w_raw[e] = keep.tile([P, PASSES, PACK, N], F32, name="w_raw%d" % e)
             nc.sync.dma_start(w_raw[e][:], w[e].rearrange("(g p j) n -> p g j n", p=P, j=PACK))
 
+        def load_half(e, g):
+            if g == 0:
+                w_raw[e] = keep.tile([P, PASSES, PACK, N], F32, name="w_raw%d" % e)
+            nc.sync.dma_start(w_raw[e][:, g], w[e].rearrange("(g p j) n -> g p j n", p=P, j=PACK)[g])
+
         def load_gate():
             nc.sync.dma_start(gate_sb[:], gate)
 
@@ -65,7 +70,8 @@ def tile_routed_moe_kernel(tc, xT, w, gate, offs, out):
         load_weights(0)
         load_weights(1)
         load_weights(2)
-        load_weights(3)
+        load_half(3, 0)
+        load_half(3, 1)
         load_gate()
 
         g4 = [keep.tile([P, PACK, SLOTS], F32, name="g4_%d" % g) for g in range(PASSES)]
@@ -202,7 +208,8 @@ def tile_routed_moe_kernel(tc, xT, w, gate, offs, out):
         multiply(0)
         multiply(1)
         interleave_weights(2, "scalar")
-        interleave_weights(3, "vector")
+        interleave_half(3, 0, "vector")
+        interleave_half(3, 1, "vector")
         sums_to_sbuf((0, 1), "scalar")
         quantize_weights(2)
         quantize_weights(3)

from contextlib import ExitStack

import concourse.mybir as mybir

K, T, E, C, N = 1024, 1024, 4, 128, 128
FLOPS = 2 * K * N * E * C

F32 = mybir.dt.float32
BF16 = mybir.dt.bfloat16
U32 = mybir.dt.uint32
U16 = mybir.dt.uint16
U8 = mybir.dt.uint8
FP8X4 = mybir.dt.float8_e4m3fn_x4
MULT = mybir.AluOpType.mult
COPY = mybir.ActivationFunctionType.Copy

P = 128
PACK = 4
PASSES = K // (P * PACK)
SLOTS = E * C
SL = 256
NSL = SLOTS // SL
EPS = SL // C
LINE = 4
SCATTERS = ((0, 1), (2, 3))


def tile_routed_moe_kernel(tc, xT, w, gate, offs, out):
    nc = tc.nc
    with ExitStack() as ctx:
        keep = ctx.enter_context(tc.tile_pool(name="keep", bufs=1))
        psum = ctx.enter_context(tc.psum_pool(name="psum", bufs=1))

        offsets = keep.tile([P, SLOTS // 16], U16, name="offsets")
        nc.sync.dma_start(offsets[:], offs)

        window = keep.tile([P, T], F32, name="window")
        nc.vector.memset(window[:], 0.0)

        planes_hbm = xT.rearrange("(g p t) n -> g p t n", p=P, t=PACK)
        plane = {}
        w_raw = {}
        gate_sb = keep.tile([P, SLOTS], F32, name="gate_sb")

        def load_plane(g, t):
            plane[g, t] = keep.tile([P, T], F32, name="plane%d%d" % (g, t))
            queue = nc.scalar if (g, t) == (0, 1) else nc.sync
            queue.dma_start(plane[g, t][:], planes_hbm[g, :, t, :])

        def load_weights(e):
            w_raw[e] = keep.tile([P, PASSES, PACK, N], F32, name="w_raw%d" % e)
            nc.sync.dma_start(w_raw[e][:], w[e].rearrange("(g p j) n -> p g j n", p=P, j=PACK))

        def load_half(e, g):
            if g == 0:
                w_raw[e] = keep.tile([P, PASSES, PACK, N], F32, name="w_raw%d" % e)
            nc.sync.dma_start(w_raw[e][:, g], w[e].rearrange("(g p j) n -> g p j n", p=P, j=PACK)[g])

        def load_gate():
            nc.sync.dma_start(gate_sb[:], gate)

        load_plane(0, 1)
        load_plane(0, 2)
        load_plane(0, 3)
        load_plane(1, 0)
        load_plane(1, 1)
        load_plane(1, 2)
        load_plane(0, 0)
        load_plane(1, 3)
        load_weights(0)
        load_weights(1)
        load_weights(2)
        load_half(3, 0)
        load_half(3, 1)
        load_gate()

        g4 = [keep.tile([P, PACK, SLOTS], F32, name="g4_%d" % g) for g in range(PASSES)]
        xg = {}
        xc = {}
        xs = {}
        for g in range(PASSES):
            for s in range(NSL):
                xg[g, s] = keep.tile([P, SL, PACK], BF16, name="xg_%d%d" % (g, s), align_bytes=64)
                xc[g, s] = keep.tile([P, SL], U32, name="xc_%d%d" % (g, s), align_bytes=64)
                xs[g, s] = keep.tile([P, SL], U8, name="xs_%d%d" % (g, s), align_bytes=64)

        def list_slice(s):
            return offsets[:, s * (SL // 16) : (s + 1) * (SL // 16)]

        def gather_all(g, t):
            nc.vector.tensor_copy(g4[g][:, t, :], plane[g, t][:].indirect(offsets[:]))

        def gather(g, t, s):
            nc.vector.tensor_copy(g4[g][:, t, s * SL : (s + 1) * SL], plane[g, t][:].indirect(list_slice(s)))

        def gather_straight(g, t, s):
            nc.vector.tensor_copy(xg[g, s][:, :, t], plane[g, t][:].indirect(list_slice(s)))

        rounded = {}

        def round_plane(g, t, engine):
            rounded[g, t] = keep.tile([P, T], BF16, name="rounded%d%d" % (g, t))
            copy_on(engine, rounded[g, t][:], plane[g, t][:])

        def gather_on_scalar(g, t, s):
            nc.scalar.activation(xg[g, s][:, :, t], rounded[g, t][:].indirect(list_slice(s)), COPY)

        def copy_on(engine, dst, src):
            if engine == "scalar":
                nc.scalar.copy(dst, src)
            elif engine == "gpsimd":
                nc.gpsimd.tensor_copy(dst, src)
            else:
                nc.vector.tensor_copy(dst, src)

        def interleave_tokens(g, s, engine, t0=0, t1=PACK):
            dst = xg[g, s][:, :, t0:t1].rearrange("p (c i) t -> p c t i", i=LINE)
            src = g4[g][:, t0:t1, s * SL : (s + 1) * SL].rearrange("p t (c i) -> p c t i", i=LINE)
            copy_on(engine, dst, src)

        def quantize_tokens(g, s):
            nc.vector.quantize_mx(
                out=xc[g, s][:].bitcast(FP8X4),
                scales=xs[g, s][:],
                in_=xg[g, s][:].rearrange("p n t -> p (n t)"),
            )

        wg = []
        wc = []
        ws = []
        for e in range(E):
            wg.append(keep.tile([P, PASSES, N, PACK], BF16, name="wg%d" % e, align_bytes=64))
            wc.append(keep.tile([P, PASSES * N], U32, name="wc%d" % e, align_bytes=64))
            ws.append(keep.tile([P, PASSES * N], U8, name="ws%d" % e, align_bytes=64))

        def interleave_weights(e, engine):
            dst = wg[e][:].rearrange("p g (c i) j -> p g c j i", i=LINE)
            src = w_raw[e][:].rearrange("p g j (c i) -> p g c j i", i=LINE)
            copy_on(engine, dst, src)

        def interleave_half(e, g, engine):
            dst = wg[e][:, g].rearrange("p (c i) j -> p c j i", i=LINE)
            src = w_raw[e][:, g].rearrange("p j (c i) -> p c j i", i=LINE)
            copy_on(engine, dst, src)

        def quantize_weights(e):
            nc.vector.quantize_mx(
                out=wc[e][:].bitcast(FP8X4),
                scales=ws[e][:],
                in_=wg[e][:].rearrange("p g n j -> p (g n j)"),
            )

        acc = {}
        y_sb = {}
        home = {}
        for experts in SCATTERS:
            acc[experts] = psum.tile([P, len(experts) * C], F32, name="acc%d" % experts[0])
            y_sb[experts] = keep.tile([P, len(experts) * C], F32, name="y_sb%d" % experts[0])
            for i, e in enumerate(experts):
                home[e] = acc[experts][:, i * C : (i + 1) * C]

        def multiply(e):
            s, c0 = e // EPS, (e % EPS) * C
            for g in range(PASSES):
                nc.tensor.matmul_mx(
                    out=home[e],
                    lhsT=wc[e][:, g * N : (g + 1) * N].bitcast(FP8X4),
                    lhsT_scale=ws[e][:, g * N : (g + 1) * N],
                    rhs=xc[g, s][:, c0 : c0 + C].bitcast(FP8X4),
                    rhs_scale=xs[g, s][:, c0 : c0 + C],
                    start=(g == 0),
                    stop=(g == PASSES - 1),
                )

        def sums_to_sbuf(experts, engine="scalar"):
            copy_on(engine, y_sb[experts][:], acc[experts][:])

        def scatter(experts):
            j0, j1 = experts[0] * C, (experts[-1] + 1) * C
            nc.vector.tensor_tensor(
                window[:].indirect(offsets[:, j0 // 16 : j1 // 16]), y_sb[experts][:], gate_sb[:, j0:j1], MULT
            )

        gather_all(0, 1)
        gather_all(0, 2)
        gather_all(0, 3)
        interleave_tokens(0, 1, "scalar", 1, 4)
        interleave_tokens(0, 0, "scalar", 1, 4)
        gather_all(1, 0)
        gather_all(1, 1)
        gather(1, 2, 0)
        gather(1, 2, 1)
        interleave_tokens(1, 0, "vector", 0, 3)
        interleave_tokens(1, 1, "vector", 0, 3)
        round_plane(0, 0, "scalar")
        gather_on_scalar(0, 0, 0)
        gather_on_scalar(0, 0, 1)
        gather_straight(1, 3, 0)
        gather_straight(1, 3, 1)
        quantize_tokens(0, 0)
        quantize_tokens(1, 0)
        quantize_tokens(0, 1)
        quantize_tokens(1, 1)
        interleave_weights(0, "scalar")
        interleave_weights(1, "vector")
        quantize_weights(0)
        quantize_weights(1)
        multiply(0)
        multiply(1)
        interleave_weights(2, "scalar")
        interleave_half(3, 0, "vector")
        interleave_half(3, 1, "vector")
        sums_to_sbuf((0, 1), "scalar")
        quantize_weights(2)
        quantize_weights(3)
        multiply(2)
        multiply(3)
        sums_to_sbuf((2, 3), "scalar")
        scatter((0, 1))
        scatter((2, 3))

        nc.sync.dma_start(out, window[:])
